import numpy as np
import ml_dtypes


def mxq(x, axis, fmt="e4m3"):
    dtype, down = {"e4m3": (ml_dtypes.float8_e4m3fn, 7), "e5m2": (ml_dtypes.float8_e5m2, 14)}[fmt]
    v = np.moveaxis(np.asarray(x, np.float32).astype(ml_dtypes.bfloat16).astype(np.float64), axis, -1)
    blocks = v.reshape(v.shape[:-1] + (-1, 32))
    amax = np.abs(blocks).max(-1, keepdims=True)
    byte = np.maximum(np.where(amax > 0, np.frexp(amax)[1] - 1 + 127, 0) - down, 1)
    scale = np.exp2(byte - 127.0)
    codes = (blocks / scale).astype(np.float32).astype(dtype).astype(np.float64)
    return np.moveaxis((codes * scale).reshape(v.shape), -1, axis)


WIDE = False


def mx_kscale(k):
    if not WIDE:
        return np.ones(k)
    levels = np.array([10, -10, 5, -5, 0])
    if k % 512:
        return np.exp2(np.random.permutation(np.resize(levels, k // 32))).repeat(32)
    a = np.empty((k // 512, 16))
    for p in range(k // 512):
        a[p, :8] = np.random.permutation(np.resize(levels, 8))
        for g in range(8):
            far = levels[np.abs(levels - a[p, g]) >= 10]
            a[p, g + 8] = far[np.random.randint(len(far))]
    return np.exp2(a.ravel()).repeat(32)


def f64(x):
    return np.asarray(x).astype(np.float64)


def striped(idx):
    return np.tile(idx.reshape(-1, 16).T, (8, 1)).astype(np.uint16)


def unstriped(offs):
    return offs[:16].T.reshape(-1).astype(np.int64)


E2M1 = np.array([0.0, 0.5, 1.0, 1.5, 2.0, 3.0, 4.0, 6.0, -0.0, -0.5, -1.0, -1.5, -2.0, -3.0, -4.0, -6.0])


def pack_weight(w, fmt):
    k, n = w.shape
    w = f64(np.asarray(w, np.float32).astype(ml_dtypes.bfloat16)).reshape(k // 32, 32, n)
    amax = np.abs(w).max(1)
    if fmt == "e4m3":
        byte = np.frexp(amax)[1] - 1 + 127 - 7
    else:
        mant, ex = np.frexp(amax / 6.0)
        byte = np.where(mant > 0.5, ex, ex - 1) + 127
    byte = np.clip(np.where(amax > 0, byte, 1), 1, 254)
    scaled = (w * np.exp2(127.0 - byte)[:, None, :]).reshape(k, n).astype(np.float32)
    by_word = np.ascontiguousarray(scaled.reshape(k // 512, 128, 4, n).transpose(0, 1, 3, 2))
    if fmt == "e4m3":
        words = by_word.astype(ml_dtypes.float8_e4m3fn).view(np.uint8)
    else:
        c = by_word.astype(ml_dtypes.float4_e2m1fn).view(np.uint8) & 0xF
        words = (c[..., 0::2] | (c[..., 1::2] << 4)).reshape(k // 512, 128, 2 * n)
    return np.ascontiguousarray(words), np.ascontiguousarray(byte.astype(np.uint8).reshape(k // 512, 16, n))


def unpack_weight(words, scales, fmt):
    g, _, n = scales.shape
    words = np.ascontiguousarray(words).reshape(g, 128, n, -1)
    if fmt == "e4m3":
        vals = words.view(ml_dtypes.float8_e4m3fn).astype(np.float64)
    else:
        nib = np.empty((g, 128, n, 4), np.uint8)
        nib[..., 0::2] = words & 0xF
        nib[..., 1::2] = words >> 4
        vals = E2M1[nib]
    vals = vals * np.repeat(np.exp2(scales.astype(np.float64) - 127.0), 8, axis=1)[..., None]
    return vals.transpose(0, 1, 3, 2).reshape(g * 512, n)


def gelu(v):
    return 0.5 * v * (1.0 + np.tanh(np.sqrt(2.0 / np.pi) * (v + 0.044715 * v**3)))


K, T, S, H, T2, P, N = 1024, 4096, 1024, 512, 2048, 1024, 768


def setup_inputs():
    n = np.random.standard_normal
    s = mx_kscale(K)[:, None]
    u = mx_kscale(H)[:, None]
    tab_words, tab_scales = pack_weight(n((K, T)) * s, "e4m3")
    w4_words, w4_scales = pack_weight(0.8 * n((H, N)) / np.sqrt(H) / u, "e2m1")
    return {
        "tab_words": tab_words, "tab_scales": tab_scales,
        "offs": striped(np.random.permutation(T)[:S]),
        "offs2": striped(np.random.permutation(T2)[:S]),
        "offs3": striped(np.random.permutation(T2)[:P]),
        "w1": (n((K, H)) / np.sqrt(K) / s * u.T).astype(np.float32),
        "wind": (0.7 * n((H, S)) * u).astype(np.float32),
        "page0": (n((H, T2)) * u).astype(np.float32),
        "w4_words": w4_words, "w4_scales": w4_scales,
        "w2": (0.7 * n((K, N)) / np.sqrt(K) / s).astype(np.float32),
        "w3": (n((H, N)) / np.sqrt(H) / u).astype(np.float32),
        "level": (0.6 * n(N)).astype(np.float32),
    }


def reference(tab_words, tab_scales, offs, offs2, offs3, w1, wind, page0, w4_words, w4_scales, w2, w3, level):
    v = unpack_weight(tab_words, tab_scales, "e4m3")[:, unstriped(offs)]
    h = (mxq(f64(w1), 0, "e4m3").T @ v) + f64(wind)
    page = f64(page0).copy()
    l2 = unstriped(offs2)
    page[:, l2] = np.maximum(page[:, l2], h)
    x = page[:, unstriped(offs3)]
    xq = mxq(x, 0, "e4m3")
    w4 = unpack_weight(w4_words, w4_scales, "e2m1")
    ya = w4.T @ xq + mxq(f64(w2), 0, "e4m3").T @ v
    yb = (mxq(f64(w3), 0, "e4m3").T @ xq) + f64(level)[:, None]
    return np.tanh(np.maximum(ya, yb))

@@ -1,0 +1,318 @@
+from contextlib import ExitStack
+
+import concourse.mybir as mybir
+from concourse.masks import make_identity
+
+K, T, S, H, T2, PICK, N = 1024, 4096, 1024, 512, 2048, 1024, 768
+
+FLOPS = 2 * K * H * S + 2 * H * N * PICK * 2 + 2 * K * N * PICK
+
+F32 = mybir.dt.float32
+BF16 = mybir.dt.bfloat16
+I32 = mybir.dt.int32
+U32 = mybir.dt.uint32
+U16 = mybir.dt.uint16
+U8 = mybir.dt.uint8
+FP8X4 = mybir.dt.float8_e4m3fn_x4
+FP4X4 = mybir.dt.float4_e2m1fn_x4
+ALU = mybir.AluOpType
+ACT = mybir.ActivationFunctionType
+
+P = 128
+PACK = 4
+K_PASS = P * PACK
+PASSES = K // K_PASS
+BANK = 512
+LIST_GROUP = 16
+CHUNK = 256
+CHUNKS = PICK // CHUNK
+PAIRS = N // (2 * P)
+HALF_N = N // 2
+ALIGN = 64
+PRODUCT_BANKS = (0, 1)
+TURNED_BANKS = (2, 3)
+FEATURE_BANKS = (4, 5)
+SUM_BANKS = (6, 7, 0, 1, 2)
+ALONE_BANKS = (3, 4, 5)
+
+
+def tile_list_zone_exposure_page_kernel(
+    tc, tab_words, tab_scales, offs, offs2, offs3, w1, wind, page0, w4_words, w4_scales, w2, w3, level, out
+):
+    nc = tc.nc
+
+    with ExitStack() as ctx:
+        pool = ctx.enter_context(tc.tile_pool(name="sbuf", bufs=1))
+        psum = ctx.enter_context(tc.psum_pool(name="psum", bufs=1))
+
+        def sbuf(name, shape, dtype, tag=None):
+            return pool.tile(shape, dtype, name=name, tag=tag or name, align_bytes=ALIGN)
+
+        def bank(name, b):
+            return psum.tile([P, BANK], F32, name=name, tag="bank%d" % b)
+
+        def entries(list_tile, first, count):
+            return list_tile[:, first // LIST_GROUP : (first + count) // LIST_GROUP]
+
+        def load(name, shape, dtype, src, tag=None):
+            t = sbuf(name, shape, dtype, tag)
+            nc.sync.dma_start(out=t[:], in_=src)
+            return t
+
+        def load_rows(name, w, a):
+            rows = w[a * K_PASS : (a + 1) * K_PASS, :]
+            return load(name, [P, PACK, w.shape[1]], F32, rows.rearrange("(p j) c -> p j c", j=PACK))
+
+        def load_words(a):
+            src = tab_words[a].rearrange("p t i -> p (t i)").bitcast(I32)
+            return load("tab_words%d" % a, [P, T], I32, src)
+
+        page_rows = page0.rearrange("(p t) c -> t p c", t=PACK)
+        wind_rows = wind.rearrange("(p t) j -> t p j", t=PACK)
+        page = [None] * PACK
+        wind_t = [None] * PACK
+
+        def load_page(t):
+            page[t] = load("page%d" % t, [P, T2], F32, page_rows[t])
+
+        def load_wind(t):
+            wind_t[t] = load("wind%d" % t, [P, S], F32, wind_rows[t])
+
+        words0 = load_words(0)
+        list1 = load("list1", [P, S // LIST_GROUP], U16, offs)
+        tab_scale_rows = sbuf("tab_scale_rows", [P, T], U8)
+        nc.vector.memset(tab_scale_rows[:].bitcast(I32), 0)
+        for q in range(4):
+            nc.sync.dma_start(
+                out=tab_scale_rows[32 * q : 32 * q + 4 * PASSES, :].bitcast(I32),
+                in_=tab_scales[:, 4 * q : 4 * q + 4, :].bitcast(I32),
+            )
+        words1 = load_words(1)
+        list2 = load("list2", [P, S // LIST_GROUP], U16, offs2)
+        load_page(0)
+        w1_raw = [load_rows("w1_raw%d" % a, w1, a) for a in range(PASSES)]
+        load_wind(0)
+        for t in (1, 2):
+            load_page(t)
+            load_wind(t)
+        list3 = load("list3", [P, PICK // LIST_GROUP], U16, offs3)
+        w3_raw = load_rows("w3_raw", w3, 0)
+        w2_raw = [load_rows("w2_raw%d" % a, w2, a) for a in range(PASSES)]
+        w4_codes = load("w4_codes", [P, 2 * N], U8, w4_words[0])
+        w4_scale_rows = sbuf("w4_scale_rows", [P, N], U8)
+        nc.vector.memset(w4_scale_rows[:].bitcast(I32), 0)
+        for q in range(4):
+            nc.sync.dma_start(
+                out=w4_scale_rows[32 * q : 32 * q + 4, :].bitcast(I32),
+                in_=w4_scales[0, 4 * q : 4 * q + 4, :].bitcast(I32),
+            )
+        load_wind(3)
+        load_page(3)
+        with nc.allow_non_contiguous_dma(reason="one level value a partition and output tile"):
+            level_cols = load("level_cols", [P, N // P], F32, level.rearrange("(i p) -> p i", p=P))
+
+        v_codes = [sbuf("v_codes%d" % a, [P, S], U32) for a in range(PASSES)]
+        v_scales = sbuf("v_scales", [P, S], U8)
+        nc.vector.tensor_copy(out=v_codes[0][:], in_=words0[:].bitcast(U32).indirect(list1[:]))
+        nc.vector.tensor_copy(out=v_scales[:], in_=tab_scale_rows[:].indirect(list1[:]))
+        nc.vector.tensor_copy(out=v_codes[1][:], in_=words1[:].bitcast(U32).indirect(list1[:]))
+
+        def v_operand(a, cols):
+            return v_codes[a][:, cols].bitcast(FP8X4), v_scales[4 * a : P, cols]
+
+        def quantize(codes, scales, grouped):
+            nc.vector.quantize_mx(out=codes.bitcast(FP8X4), scales=scales, in_=grouped)
+
+        w1_codes = [sbuf("w1_codes%d" % a, [P, H], U32) for a in range(PASSES)]
+        w1_scales = [sbuf("w1_scales%d" % a, [P, H], U8) for a in range(PASSES)]
+
+        def quantize_w1(a, t0, t1):
+            grouped = sbuf("w1_bf%d_%d" % (a, t0), [P, t1 - t0, P, PACK], BF16)
+            nc.scalar.copy(
+                out=grouped[:].rearrange("p t m j -> p m j t"),
+                in_=w1_raw[a][:].rearrange("p j (m t) -> p m j t", t=PACK)[:, :, :, t0:t1],
+            )
+            cols = slice(t0 * P, t1 * P)
+            quantize(w1_codes[a][:, cols], w1_scales[a][:, cols], grouped[:].rearrange("p t m j -> p (t m j)"))
+
+        def quantize_weight(name, raw):
+            codes = sbuf(name + "_codes", [P, N], U32)
+            scales = sbuf(name + "_scales", [P, N], U8)
+            for u in range(2):
+                cols = slice(u * HALF_N, (u + 1) * HALF_N)
+                grouped = sbuf("%s_bf%d" % (name, u), [P, HALF_N, PACK], BF16)
+                nc.scalar.copy(
+                    out=grouped[:].rearrange("p (c i) j -> p c j i", i=4),
+                    in_=raw[:, :, cols].rearrange("p j (c i) -> p c j i", i=4),
+                )
+                quantize(codes[:, cols], scales[:, cols], grouped[:].rearrange("p c j -> p (c j)"))
+            return codes, scales
+
+        def fetch_standing(t):
+            standing = sbuf("standing%d" % t, [P, S], F32, "standing%d" % (t % 2))
+            nc.vector.tensor_copy(out=standing[:], in_=page[t][:].indirect(list2[:]))
+            return standing
+
+        identity = sbuf("identity", [P, P], F32)
+        make_identity(nc, identity[:])
+        halves = [slice(u * BANK, (u + 1) * BANK) for u in range(S // BANK)]
+
+        def first_product(t, u, b):
+            acc = bank("product%d_%d" % (t, u), b)
+            for a in range(PASSES):
+                rhs, rhs_scale = v_operand(a, halves[u])
+                nc.tensor.matmul_mx(
+                    out=acc[:],
+                    lhsT=w1_codes[a][:, t * P : (t + 1) * P].bitcast(FP8X4),
+                    lhsT_scale=w1_scales[a][:, t * P : (t + 1) * P],
+                    rhs=rhs,
+                    rhs_scale=rhs_scale,
+                    start=(a == 0),
+                    stop=(a == PASSES - 1),
+                )
+            return acc
+
+        def feature_on_vector(t):
+            feature = sbuf("feature%d" % t, [P, S], F32, "feature0")
+            for u, cols in enumerate(halves):
+                acc = first_product(t, u, FEATURE_BANKS[u])
+                nc.vector.tensor_tensor(out=feature[:, cols], in0=acc[:], in1=wind_t[t][:, cols], op=ALU.add)
+            return [feature[:, cols] for cols in halves]
+
+        def feature_on_tensor(t):
+            product = sbuf("product%d" % t, [P, S], F32, "feature1")
+            turned = sbuf("turned%d" % t, [P, S], F32, "turned")
+            for u, cols in enumerate(halves):
+                nc.scalar.copy(out=product[:, cols], in_=first_product(t, u, PRODUCT_BANKS[u])[:])
+            for u, cols in enumerate(halves):
+                acc = bank("turned%d_%d" % (t, u), TURNED_BANKS[u])
+                for b in range(BANK // P):
+                    block = slice(u * BANK + b * P, u * BANK + (b + 1) * P)
+                    for term, first in ((product, True), (wind_t[t], False)):
+                        nc.tensor.matmul(
+                            acc[:, b * P : (b + 1) * P],
+                            lhsT=term[:, block],
+                            rhs=identity[:],
+                            is_transpose=True,
+                            start=first,
+                            stop=not first,
+                        )
+                nc.scalar.copy(out=turned[:, cols], in_=acc[:])
+            feature = []
+            for u, cols in enumerate(halves):
+                acc = bank("feature%d_%d" % (t, u), FEATURE_BANKS[u])
+                for b in range(BANK // P):
+                    block = slice(u * BANK + b * P, u * BANK + (b + 1) * P)
+                    nc.tensor.transpose(acc[:, b * P : (b + 1) * P], turned[:, block], identity[:])
+                feature.append(acc[:])
+            return feature
+
+        def update_page(t, standing, feature):
+            larger = sbuf("larger%d" % t, [P, S], F32, "larger%d" % (t % 2))
+            for u, cols in enumerate(halves):
+                nc.vector.tensor_tensor(out=larger[:, cols], in0=feature[u], in1=standing[:, cols], op=ALU.max)
+            for u, cols in enumerate(halves):
+                nc.vector.tensor_copy(out=page[t][:].indirect(entries(list2, u * BANK, BANK)), in_=larger[:, cols])
+
+        standing = fetch_standing(0)
+        quantize_w1(0, 0, PACK)
+        quantize_w1(1, 0, 1)
+        quantize_w1(1, 1, PACK)
+        update_page(0, standing, feature_on_vector(0))
+        for t in (1, 2):
+            update_page(t, fetch_standing(t), feature_on_tensor(t))
+        w3_codes, w3_scales = quantize_weight("w3", w3_raw)
+        w2_q = [quantize_weight("w2_%d" % a, w2_raw[a]) for a in range(PASSES)]
+        update_page(3, fetch_standing(3), feature_on_tensor(3))
+
+        x_codes = sbuf("x_codes", [P, PICK], U32)
+        x_scales = sbuf("x_scales", [P, PICK], U8)
+        out_tiles = out.rearrange("(i p) j -> p i j", p=P)
+        fetched = [None] * CHUNKS
+
+        def fetch_zones(c):
+            fetched[c] = sbuf("zones%d" % c, [P, PACK, CHUNK], F32, "larger%d" % (c % 2))
+            for t in range(PACK):
+                nc.vector.tensor_copy(out=fetched[c][:, t, :], in_=page[t][:].indirect(entries(list3, c * CHUNK, CHUNK)))
+
+        def quantize_zones(c):
+            cols = slice(c * CHUNK, (c + 1) * CHUNK)
+            grouped = sbuf("x_bf%d" % c, [P, CHUNK, PACK], BF16, "x_bf%d" % (c % 2))
+            nc.scalar.copy(
+                out=grouped[:].rearrange("p (c i) t -> p c t i", i=4),
+                in_=fetched[c][:].rearrange("p t (c i) -> p c t i", i=4),
+            )
+            quantize(x_codes[:, cols], x_scales[:, cols], grouped[:].rearrange("p c t -> p (c t)"))
+
+        def score(c):
+            cols = slice(c * CHUNK, (c + 1) * CHUNK)
+            x_operand = x_codes[:, cols].bitcast(FP8X4)
+            result = sbuf("result%d" % c, [P, N // P, CHUNK], F32, "tab_words%d" % (c % 2))
+            for pair in range(PAIRS):
+                unit = c * PAIRS + pair
+                together = bank("together%d" % unit, SUM_BANKS[unit % len(SUM_BANKS)])
+                alone = bank("alone%d" % unit, ALONE_BANKS[unit % len(ALONE_BANKS)])
+                for e in range(2):
+                    n_cols = slice((2 * pair + e) * P, (2 * pair + e + 1) * P)
+                    for a in range(PASSES):
+                        rhs, rhs_scale = v_operand(a, cols)
+                        nc.tensor.matmul_mx(
+                            out=together[:, e * CHUNK : (e + 1) * CHUNK],
+                            lhsT=w2_q[a][0][:, n_cols].bitcast(FP8X4),
+                            lhsT_scale=w2_q[a][1][:, n_cols],
+                            rhs=rhs,
+                            rhs_scale=rhs_scale,
+                            start=(e == 0 and a == 0),
+                            stop=False,
+                        )
+                for e in range(2):
+                    i = 2 * pair + e
+                    nc.tensor.matmul_mx(
+                        out=together[:, e * CHUNK : (e + 1) * CHUNK],
+                        lhsT=w4_codes[:, 2 * i * P : 2 * (i + 1) * P].bitcast(FP4X4),
+                        lhsT_scale=w4_scale_rows[:, i * P : (i + 1) * P],
+                        rhs=x_operand,
+                        rhs_scale=x_scales[:, cols],
+                        start=False,
+                        stop=(e == 1),
+                    )
+                for e in range(2):
+                    i = 2 * pair + e
+                    nc.tensor.matmul_mx(
+                        out=alone[:, e * CHUNK : (e + 1) * CHUNK],
+                        lhsT=w3_codes[:, i * P : (i + 1) * P].bitcast(FP8X4),
+                        lhsT_scale=w3_scales[:, i * P : (i + 1) * P],
+                        rhs=x_operand,
+                        rhs_scale=x_scales[:, cols],
+                        start=True,
+                        stop=True,
+                    )
+                tanh_together = sbuf("tanh_together%d" % unit, [P, BANK], F32, "standing%d" % (unit % 2))
+                tanh_alone = sbuf("tanh_alone%d" % unit, [P, BANK], F32, "feature%d" % (unit % 2))
+                nc.scalar.activation(out=tanh_together[:], in_=together[:], func=ACT.Tanh)
+                for e in range(2):
+                    i = 2 * pair + e
+                    nc.scalar.activation(
+                        out=tanh_alone[:, e * CHUNK : (e + 1) * CHUNK],
+                        in_=alone[:, e * CHUNK : (e + 1) * CHUNK],
+                        func=ACT.Tanh,
+                        bias=level_cols[:, i : i + 1],
+                    )
+                nc.vector.tensor_tensor(
+                    out=result[:, 2 * pair : 2 * pair + 2, :].rearrange("p e j -> p (e j)"),
+                    in0=tanh_together[:],
+                    in1=tanh_alone[:],
+                    op=ALU.max,
+                )
+                nc.sync.dma_start(
+                    out=out_tiles[:, 2 * pair : 2 * pair + 2, cols], in_=result[:, 2 * pair : 2 * pair + 2, :]
+                )
+
+        fetch_zones(0)
+        for c in range(CHUNKS + 1):
+            if c + 1 < CHUNKS:
+                fetch_zones(c + 1)
+            if c < CHUNKS:
+                quantize_zones(c)
+            if c >= 1:
+                score(c - 1)

@@ -34,6 +34,7 @@ TURNED_BANKS = (2, 3)
 FEATURE_BANKS = (4, 5)
 SUM_BANKS = (6, 7, 0, 1, 2)
 ALONE_BANKS = (3, 4, 5)
+SCORE_TAGS = ("w2_raw0", "w2_raw1", "w3_raw")
 
 
 def tile_list_zone_exposure_page_kernel(
@@ -87,17 +88,16 @@ def tile_list_zone_exposure_page_kernel(
                 out=tab_scale_rows[32 * q : 32 * q + 4 * PASSES, :].bitcast(I32),
                 in_=tab_scales[:, 4 * q : 4 * q + 4, :].bitcast(I32),
             )
+        w1_raw = [load_rows("w1_raw%d" % a, w1, a) for a in range(PASSES)]
         words1 = load_words(1)
         list2 = load("list2", [P, S // LIST_GROUP], U16, offs2)
-        load_page(0)
-        w1_raw = [load_rows("w1_raw%d" % a, w1, a) for a in range(PASSES)]
-        load_wind(0)
-        for t in (1, 2):
+        for t in range(PACK - 1):
             load_page(t)
             load_wind(t)
+        load_wind(PACK - 1)
         list3 = load("list3", [P, PICK // LIST_GROUP], U16, offs3)
-        w3_raw = load_rows("w3_raw", w3, 0)
         w2_raw = [load_rows("w2_raw%d" % a, w2, a) for a in range(PASSES)]
+        w3_raw = load_rows("w3_raw", w3, 0)
         w4_codes = load("w4_codes", [P, 2 * N], U8, w4_words[0])
         w4_scale_rows = sbuf("w4_scale_rows", [P, N], U8)
         nc.vector.memset(w4_scale_rows[:].bitcast(I32), 0)
@@ -106,16 +106,15 @@ def tile_list_zone_exposure_page_kernel(
                 out=w4_scale_rows[32 * q : 32 * q + 4, :].bitcast(I32),
                 in_=w4_scales[0, 4 * q : 4 * q + 4, :].bitcast(I32),
             )
-        load_wind(3)
-        load_page(3)
+        load_page(PACK - 1)
         with nc.allow_non_contiguous_dma(reason="one level value a partition and output tile"):
             level_cols = load("level_cols", [P, N // P], F32, level.rearrange("(i p) -> p i", p=P))
 
+        halves = [slice(u * BANK, (u + 1) * BANK) for u in range(S // BANK)]
         v_codes = [sbuf("v_codes%d" % a, [P, S], U32) for a in range(PASSES)]
         v_scales = sbuf("v_scales", [P, S], U8)
         nc.vector.tensor_copy(out=v_codes[0][:], in_=words0[:].bitcast(U32).indirect(list1[:]))
         nc.vector.tensor_copy(out=v_scales[:], in_=tab_scale_rows[:].indirect(list1[:]))
-        nc.vector.tensor_copy(out=v_codes[1][:], in_=words1[:].bitcast(U32).indirect(list1[:]))
 
         def v_operand(a, cols):
             return v_codes[a][:, cols].bitcast(FP8X4), v_scales[4 * a : P, cols]
@@ -126,14 +125,13 @@ def tile_list_zone_exposure_page_kernel(
         w1_codes = [sbuf("w1_codes%d" % a, [P, H], U32) for a in range(PASSES)]
         w1_scales = [sbuf("w1_scales%d" % a, [P, H], U8) for a in range(PASSES)]
 
-        def quantize_w1(a, t0, t1):
-            grouped = sbuf("w1_bf%d_%d" % (a, t0), [P, t1 - t0, P, PACK], BF16)
+        def quantize_w1(a):
+            grouped = sbuf("w1_bf%d" % a, [P, PACK, P, PACK], BF16)
             nc.scalar.copy(
                 out=grouped[:].rearrange("p t m j -> p m j t"),
-                in_=w1_raw[a][:].rearrange("p j (m t) -> p m j t", t=PACK)[:, :, :, t0:t1],
+                in_=w1_raw[a][:].rearrange("p j (m t) -> p m j t", t=PACK),
             )
-            cols = slice(t0 * P, t1 * P)
-            quantize(w1_codes[a][:, cols], w1_scales[a][:, cols], grouped[:].rearrange("p t m j -> p (t m j)"))
+            quantize(w1_codes[a][:], w1_scales[a][:], grouped[:].rearrange("p t m j -> p (t m j)"))
 
         def quantize_weight(name, raw):
             codes = sbuf(name + "_codes", [P, N], U32)
@@ -155,7 +153,6 @@ def tile_list_zone_exposure_page_kernel(
 
         identity = sbuf("identity", [P, P], F32)
         make_identity(nc, identity[:])
-        halves = [slice(u * BANK, (u + 1) * BANK) for u in range(S // BANK)]
 
         def first_product(t, u, b):
             acc = bank("product%d_%d" % (t, u), b)
@@ -211,18 +208,19 @@ def tile_list_zone_exposure_page_kernel(
             larger = sbuf("larger%d" % t, [P, S], F32, "larger%d" % (t % 2))
             for u, cols in enumerate(halves):
                 nc.vector.tensor_tensor(out=larger[:, cols], in0=feature[u], in1=standing[:, cols], op=ALU.max)
-            for u, cols in enumerate(halves):
-                nc.vector.tensor_copy(out=page[t][:].indirect(entries(list2, u * BANK, BANK)), in_=larger[:, cols])
+            nc.vector.tensor_copy(out=page[t][:].indirect(list2[:]), in_=larger[:])
 
-        standing = fetch_standing(0)
-        quantize_w1(0, 0, PACK)
-        quantize_w1(1, 0, 1)
-        quantize_w1(1, 1, PACK)
-        update_page(0, standing, feature_on_vector(0))
+        for a in range(PASSES):
+            quantize_w1(a)
+        for u, cols in enumerate(halves):
+            nc.vector.tensor_copy(
+                out=v_codes[1][:, cols], in_=words1[:].bitcast(U32).indirect(entries(list1, u * BANK, BANK))
+            )
+        update_page(0, fetch_standing(0), feature_on_vector(0))
         for t in (1, 2):
             update_page(t, fetch_standing(t), feature_on_tensor(t))
-        w3_codes, w3_scales = quantize_weight("w3", w3_raw)
         w2_q = [quantize_weight("w2_%d" % a, w2_raw[a]) for a in range(PASSES)]
+        w3_codes, w3_scales = quantize_weight("w3", w3_raw)
         update_page(3, fetch_standing(3), feature_on_tensor(3))
 
         x_codes = sbuf("x_codes", [P, PICK], U32)
@@ -238,7 +236,7 @@ def tile_list_zone_exposure_page_kernel(
         def quantize_zones(c):
             cols = slice(c * CHUNK, (c + 1) * CHUNK)
             grouped = sbuf("x_bf%d" % c, [P, CHUNK, PACK], BF16, "x_bf%d" % (c % 2))
-            nc.scalar.copy(
+            nc.vector.tensor_copy(
                 out=grouped[:].rearrange("p (c i) t -> p c t i", i=4),
                 in_=fetched[c][:].rearrange("p t (c i) -> p c t i", i=4),
             )
@@ -248,6 +246,7 @@ def tile_list_zone_exposure_page_kernel(
             cols = slice(c * CHUNK, (c + 1) * CHUNK)
             x_operand = x_codes[:, cols].bitcast(FP8X4)
             result = sbuf("result%d" % c, [P, N // P, CHUNK], F32, "tab_words%d" % (c % 2))
+            scores = sbuf("scores%d" % c, [P, 2, PAIRS, BANK], F32, SCORE_TAGS[c % len(SCORE_TAGS)])
             for pair in range(PAIRS):
                 unit = c * PAIRS + pair
                 together = bank("together%d" % unit, SUM_BANKS[unit % len(SUM_BANKS)])
@@ -287,9 +286,9 @@ def tile_list_zone_exposure_page_kernel(
                         start=True,
                         stop=True,
                     )
-                tanh_together = sbuf("tanh_together%d" % unit, [P, BANK], F32, "standing%d" % (unit % 2))
-                tanh_alone = sbuf("tanh_alone%d" % unit, [P, BANK], F32, "feature%d" % (unit % 2))
-                nc.scalar.activation(out=tanh_together[:], in_=together[:], func=ACT.Tanh)
+                tanh_together = scores[:, 0, pair, :]
+                tanh_alone = scores[:, 1, pair, :]
+                nc.scalar.activation(out=tanh_together, in_=together[:], func=ACT.Tanh)
                 for e in range(2):
                     i = 2 * pair + e
                     nc.scalar.activation(
@@ -300,19 +299,17 @@ def tile_list_zone_exposure_page_kernel(
                     )
                 nc.vector.tensor_tensor(
                     out=result[:, 2 * pair : 2 * pair + 2, :].rearrange("p e j -> p (e j)"),
-                    in0=tanh_together[:],
-                    in1=tanh_alone[:],
+                    in0=tanh_together,
+                    in1=tanh_alone,
                     op=ALU.max,
                 )
                 nc.sync.dma_start(
                     out=out_tiles[:, 2 * pair : 2 * pair + 2, cols], in_=result[:, 2 * pair : 2 * pair + 2, :]
                 )
 
-        fetch_zones(0)
         for c in range(CHUNKS + 1):
-            if c + 1 < CHUNKS:
-                fetch_zones(c + 1)
             if c < CHUNKS:
+                fetch_zones(c)
                 quantize_zones(c)
             if c >= 1:
                 score(c - 1)

@@ -34,7 +34,7 @@ TURNED_BANKS = (2, 3)
 FEATURE_BANKS = (4, 5)
 SUM_BANKS = (6, 7, 0, 1, 2)
 ALONE_BANKS = (3, 4, 5)
-SCORE_TAGS = ("w2_raw0", "w2_raw1", "w3_raw")
+SCORE_TAGS = ("w2_raw0", "w2_raw1", "w3_raw", "tab_words1")
 
 
 def tile_list_zone_exposure_page_kernel(
@@ -79,16 +79,22 @@ def tile_list_zone_exposure_page_kernel(
         def load_wind(t):
             wind_t[t] = load("wind%d" % t, [P, S], F32, wind_rows[t])
 
-        words0 = load_words(0)
-        list1 = load("list1", [P, S // LIST_GROUP], U16, offs)
         tab_scale_rows = sbuf("tab_scale_rows", [P, T], U8)
         nc.vector.memset(tab_scale_rows[:].bitcast(I32), 0)
-        for q in range(4):
-            nc.sync.dma_start(
-                out=tab_scale_rows[32 * q : 32 * q + 4 * PASSES, :].bitcast(I32),
-                in_=tab_scales[:, 4 * q : 4 * q + 4, :].bitcast(I32),
-            )
-        w1_raw = [load_rows("w1_raw%d" % a, w1, a) for a in range(PASSES)]
+
+        def load_tab_scales(a, quadrants):
+            for q in quadrants:
+                nc.sync.dma_start(
+                    out=tab_scale_rows[32 * q + 4 * a : 32 * q + 4 * a + 4, :].bitcast(I32),
+                    in_=tab_scales[a, 4 * q : 4 * q + 4, :].bitcast(I32),
+                )
+
+        words0 = load_words(0)
+        list1 = load("list1", [P, S // LIST_GROUP], U16, offs)
+        w1_raw = []
+        for a in range(PASSES):
+            load_tab_scales(a, range(4))
+            w1_raw.append(load_rows("w1_raw%d" % a, w1, a))
         words1 = load_words(1)
         list2 = load("list2", [P, S // LIST_GROUP], U16, offs2)
         for t in range(PACK - 1):
@@ -245,8 +251,7 @@ def tile_list_zone_exposure_page_kernel(
         def score(c):
             cols = slice(c * CHUNK, (c + 1) * CHUNK)
             x_operand = x_codes[:, cols].bitcast(FP8X4)
-            result = sbuf("result%d" % c, [P, N // P, CHUNK], F32, "tab_words%d" % (c % 2))
-            scores = sbuf("scores%d" % c, [P, 2, PAIRS, BANK], F32, SCORE_TAGS[c % len(SCORE_TAGS)])
+            scores = sbuf("scores%d" % c, [P, 2, PAIRS, BANK], F32, SCORE_TAGS[c])
             for pair in range(PAIRS):
                 unit = c * PAIRS + pair
                 together = bank("together%d" % unit, SUM_BANKS[unit % len(SUM_BANKS)])
@@ -297,15 +302,20 @@ def tile_list_zone_exposure_page_kernel(
                         func=ACT.Tanh,
                         bias=level_cols[:, i : i + 1],
                     )
-                nc.vector.tensor_tensor(
-                    out=result[:, 2 * pair : 2 * pair + 2, :].rearrange("p e j -> p (e j)"),
-                    in0=tanh_together,
-                    in1=tanh_alone,
-                    op=ALU.max,
-                )
-                nc.sync.dma_start(
-                    out=out_tiles[:, 2 * pair : 2 * pair + 2, cols], in_=result[:, 2 * pair : 2 * pair + 2, :]
-                )
+                step = 1 if unit == CHUNKS * PAIRS - 1 else 2
+                for e in range(0, 2, step):
+                    tiles = slice(2 * pair + e, 2 * pair + e + step)
+                    part = slice(e * CHUNK, (e + step) * CHUNK)
+                    nc.vector.tensor_tensor(
+                        out=tanh_together[:, part],
+                        in0=tanh_together[:, part],
+                        in1=tanh_alone[:, part],
+                        op=ALU.max,
+                    )
+                    nc.sync.dma_start(
+                        out=out_tiles[:, tiles, cols],
+                        in_=tanh_together[:, part].rearrange("p (e j) -> p e j", j=CHUNK),
+                    )
 
         for c in range(CHUNKS + 1):
             if c < CHUNKS:

@@ -31,9 +31,11 @@ HALF_N = N // 2
 ALIGN = 64
 PRODUCT_BANKS = (0, 1)
 TURNED_BANKS = (2, 3)
-FEATURE_BANKS = (4, 5)
-SUM_BANKS = (6, 7, 0, 1, 2)
-ALONE_BANKS = (3, 4, 5)
+FEATURE_BANKS = ((4, 5), (6, 7), (4, 5), (0, 1))
+SUM_BANKS = (2, 3, 6, 7, 4)
+ALONE_BANKS = (5, 0, 1)
+PRODUCT_TAGS = ("product", "w1_raw0", "w1_raw1")
+TURNED_TAGS = ("turned", "tab_words0", "tab_words1")
 SCORE_TAGS = ("w2_raw0", "w2_raw1", "w3_raw", "tab_words1")
 
 
@@ -79,22 +81,16 @@ def tile_list_zone_exposure_page_kernel(
         def load_wind(t):
             wind_t[t] = load("wind%d" % t, [P, S], F32, wind_rows[t])
 
-        tab_scale_rows = sbuf("tab_scale_rows", [P, T], U8)
-        nc.vector.memset(tab_scale_rows[:].bitcast(I32), 0)
-
-        def load_tab_scales(a, quadrants):
-            for q in quadrants:
-                nc.sync.dma_start(
-                    out=tab_scale_rows[32 * q + 4 * a : 32 * q + 4 * a + 4, :].bitcast(I32),
-                    in_=tab_scales[a, 4 * q : 4 * q + 4, :].bitcast(I32),
-                )
-
         words0 = load_words(0)
         list1 = load("list1", [P, S // LIST_GROUP], U16, offs)
-        w1_raw = []
-        for a in range(PASSES):
-            load_tab_scales(a, range(4))
-            w1_raw.append(load_rows("w1_raw%d" % a, w1, a))
+        tab_scale_rows = sbuf("tab_scale_rows", [P, T], U8)
+        nc.vector.memset(tab_scale_rows[:].bitcast(I32), 0)
+        for q in range(4):
+            nc.sync.dma_start(
+                out=tab_scale_rows[32 * q : 32 * q + 4 * PASSES, :].bitcast(I32),
+                in_=tab_scales[:, 4 * q : 4 * q + 4, :].bitcast(I32),
+            )
+        w1_raw = [load_rows("w1_raw%d" % a, w1, a) for a in range(PASSES)]
         words1 = load_words(1)
         list2 = load("list2", [P, S // LIST_GROUP], U16, offs2)
         for t in range(PACK - 1):
@@ -131,9 +127,9 @@ def tile_list_zone_exposure_page_kernel(
         w1_codes = [sbuf("w1_codes%d" % a, [P, H], U32) for a in range(PASSES)]
         w1_scales = [sbuf("w1_scales%d" % a, [P, H], U8) for a in range(PASSES)]
 
-        def quantize_w1(a):
+        def quantize_w1(a, copy):
             grouped = sbuf("w1_bf%d" % a, [P, PACK, P, PACK], BF16)
-            nc.scalar.copy(
+            copy(
                 out=grouped[:].rearrange("p t m j -> p m j t"),
                 in_=w1_raw[a][:].rearrange("p j (m t) -> p m j t", t=PACK),
             )
@@ -178,13 +174,13 @@ def tile_list_zone_exposure_page_kernel(
         def feature_on_vector(t):
             feature = sbuf("feature%d" % t, [P, S], F32, "feature0")
             for u, cols in enumerate(halves):
-                acc = first_product(t, u, FEATURE_BANKS[u])
+                acc = first_product(t, u, FEATURE_BANKS[t][u])
                 nc.vector.tensor_tensor(out=feature[:, cols], in0=acc[:], in1=wind_t[t][:, cols], op=ALU.add)
             return [feature[:, cols] for cols in halves]
 
         def feature_on_tensor(t):
-            product = sbuf("product%d" % t, [P, S], F32, "feature1")
-            turned = sbuf("turned%d" % t, [P, S], F32, "turned")
+            product = sbuf("product%d" % t, [P, S], F32, PRODUCT_TAGS[t - 1])
+            turned = sbuf("turned%d" % t, [P, S], F32, TURNED_TAGS[t - 1])
             for u, cols in enumerate(halves):
                 nc.scalar.copy(out=product[:, cols], in_=first_product(t, u, PRODUCT_BANKS[u])[:])
             for u, cols in enumerate(halves):
@@ -203,7 +199,7 @@ def tile_list_zone_exposure_page_kernel(
                 nc.scalar.copy(out=turned[:, cols], in_=acc[:])
             feature = []
             for u, cols in enumerate(halves):
-                acc = bank("feature%d_%d" % (t, u), FEATURE_BANKS[u])
+                acc = bank("feature%d_%d" % (t, u), FEATURE_BANKS[t][u])
                 for b in range(BANK // P):
                     block = slice(u * BANK + b * P, u * BANK + (b + 1) * P)
                     nc.tensor.transpose(acc[:, b * P : (b + 1) * P], turned[:, block], identity[:])
@@ -216,18 +212,19 @@ def tile_list_zone_exposure_page_kernel(
                 nc.vector.tensor_tensor(out=larger[:, cols], in0=feature[u], in1=standing[:, cols], op=ALU.max)
             nc.vector.tensor_copy(out=page[t][:].indirect(list2[:]), in_=larger[:])
 
-        for a in range(PASSES):
-            quantize_w1(a)
+        quantize_w1(0, nc.scalar.copy)
+        quantize_w1(1, nc.vector.tensor_copy)
         for u, cols in enumerate(halves):
             nc.vector.tensor_copy(
                 out=v_codes[1][:, cols], in_=words1[:].bitcast(U32).indirect(entries(list1, u * BANK, BANK))
             )
         update_page(0, fetch_standing(0), feature_on_vector(0))
+        features = {t: feature_on_tensor(t) for t in range(1, PACK)}
         for t in (1, 2):
-            update_page(t, fetch_standing(t), feature_on_tensor(t))
+            update_page(t, fetch_standing(t), features[t])
         w2_q = [quantize_weight("w2_%d" % a, w2_raw[a]) for a in range(PASSES)]
         w3_codes, w3_scales = quantize_weight("w3", w3_raw)
-        update_page(3, fetch_standing(3), feature_on_tensor(3))
+        update_page(3, fetch_standing(3), features[3])
 
         x_codes = sbuf("x_codes", [P, PICK], U32)
         x_scales = sbuf("x_scales", [P, PICK], U8)
@@ -248,27 +245,34 @@ def tile_list_zone_exposure_page_kernel(
             )
             quantize(x_codes[:, cols], x_scales[:, cols], grouped[:].rearrange("p c t -> p (c t)"))
 
+        open_sums = []
+
+        def open_sum(unit):
+            c, pair = divmod(unit, PAIRS)
+            together = bank("together%d" % unit, SUM_BANKS[unit % len(SUM_BANKS)])
+            for e in range(2):
+                n_cols = slice((2 * pair + e) * P, (2 * pair + e + 1) * P)
+                for a in range(PASSES):
+                    rhs, rhs_scale = v_operand(a, slice(c * CHUNK, (c + 1) * CHUNK))
+                    nc.tensor.matmul_mx(
+                        out=together[:, e * CHUNK : (e + 1) * CHUNK],
+                        lhsT=w2_q[a][0][:, n_cols].bitcast(FP8X4),
+                        lhsT_scale=w2_q[a][1][:, n_cols],
+                        rhs=rhs,
+                        rhs_scale=rhs_scale,
+                        start=(e == 0 and a == 0),
+                        stop=False,
+                    )
+            open_sums.append(together)
+
         def score(c):
             cols = slice(c * CHUNK, (c + 1) * CHUNK)
             x_operand = x_codes[:, cols].bitcast(FP8X4)
             scores = sbuf("scores%d" % c, [P, 2, PAIRS, BANK], F32, SCORE_TAGS[c])
             for pair in range(PAIRS):
                 unit = c * PAIRS + pair
-                together = bank("together%d" % unit, SUM_BANKS[unit % len(SUM_BANKS)])
+                together = open_sums[unit]
                 alone = bank("alone%d" % unit, ALONE_BANKS[unit % len(ALONE_BANKS)])
-                for e in range(2):
-                    n_cols = slice((2 * pair + e) * P, (2 * pair + e + 1) * P)
-                    for a in range(PASSES):
-                        rhs, rhs_scale = v_operand(a, cols)
-                        nc.tensor.matmul_mx(
-                            out=together[:, e * CHUNK : (e + 1) * CHUNK],
-                            lhsT=w2_q[a][0][:, n_cols].bitcast(FP8X4),
-                            lhsT_scale=w2_q[a][1][:, n_cols],
-                            rhs=rhs,
-                            rhs_scale=rhs_scale,
-                            start=(e == 0 and a == 0),
-                            stop=False,
-                        )
                 for e in range(2):
                     i = 2 * pair + e
                     nc.tensor.matmul_mx(
@@ -291,6 +295,8 @@ def tile_list_zone_exposure_page_kernel(
                         start=True,
                         stop=True,
                     )
+                if unit >= 1 and len(open_sums) < CHUNKS * PAIRS:
+                    open_sum(len(open_sums))
                 tanh_together = scores[:, 0, pair, :]
                 tanh_alone = scores[:, 1, pair, :]
                 nc.scalar.activation(out=tanh_together, in_=together[:], func=ACT.Tanh)
@@ -317,6 +323,8 @@ def tile_list_zone_exposure_page_kernel(
                         in_=tanh_together[:, part].rearrange("p (e j) -> p e j", j=CHUNK),
                     )
 
+        for unit in range(len(SUM_BANKS)):
+            open_sum(unit)
         for c in range(CHUNKS + 1):
             if c < CHUNKS:
                 fetch_zones(c)

@@ -213,7 +213,7 @@ def tile_list_zone_exposure_page_kernel(
             nc.vector.tensor_copy(out=page[t][:].indirect(list2[:]), in_=larger[:])
 
         quantize_w1(0, nc.scalar.copy)
-        quantize_w1(1, nc.vector.tensor_copy)
+        quantize_w1(1, nc.scalar.copy)
         for u, cols in enumerate(halves):
             nc.vector.tensor_copy(
                 out=v_codes[1][:, cols], in_=words1[:].bitcast(U32).indirect(entries(list1, u * BANK, BANK))
@@ -239,7 +239,8 @@ def tile_list_zone_exposure_page_kernel(
         def quantize_zones(c):
             cols = slice(c * CHUNK, (c + 1) * CHUNK)
             grouped = sbuf("x_bf%d" % c, [P, CHUNK, PACK], BF16, "x_bf%d" % (c % 2))
-            nc.vector.tensor_copy(
+            copy = nc.scalar.copy if c in (0, 1) else nc.vector.tensor_copy
+            copy(
                 out=grouped[:].rearrange("p (c i) t -> p c t i", i=4),
                 in_=fetched[c][:].rearrange("p t (c i) -> p c t i", i=4),
             )
@@ -271,6 +272,8 @@ def tile_list_zone_exposure_page_kernel(
             scores = sbuf("scores%d" % c, [P, 2, PAIRS, BANK], F32, SCORE_TAGS[c])
             for pair in range(PAIRS):
                 unit = c * PAIRS + pair
+                if unit == len(open_sums):
+                    open_sum(unit)
                 together = open_sums[unit]
                 alone = bank("alone%d" % unit, ALONE_BANKS[unit % len(ALONE_BANKS)])
                 for e in range(2):
@@ -295,8 +298,6 @@ def tile_list_zone_exposure_page_kernel(
                         start=True,
                         stop=True,
                     )
-                if unit >= 1 and len(open_sums) < CHUNKS * PAIRS:
-                    open_sum(len(open_sums))
                 tanh_together = scores[:, 0, pair, :]
                 tanh_alone = scores[:, 1, pair, :]
                 nc.scalar.activation(out=tanh_together, in_=together[:], func=ACT.Tanh)

from contextlib import ExitStack

import concourse.mybir as mybir
from concourse.masks import make_identity

K, T, S, H, T2, PICK, N = 1024, 4096, 1024, 512, 2048, 1024, 768

FLOPS = 2 * K * H * S + 2 * H * N * PICK * 2 + 2 * K * N * PICK

F32 = mybir.dt.float32
BF16 = mybir.dt.bfloat16
I32 = mybir.dt.int32
U32 = mybir.dt.uint32
U16 = mybir.dt.uint16
U8 = mybir.dt.uint8
FP8X4 = mybir.dt.float8_e4m3fn_x4
FP4X4 = mybir.dt.float4_e2m1fn_x4
ALU = mybir.AluOpType
ACT = mybir.ActivationFunctionType

P = 128
PACK = 4
K_PASS = P * PACK
PASSES = K // K_PASS
BANK = 512
LIST_GROUP = 16
CHUNK = 256
CHUNKS = PICK // CHUNK
PAIRS = N // (2 * P)
HALF_N = N // 2
ALIGN = 64
PRODUCT_BANKS = (0, 1)
TURNED_BANKS = (2, 3)
FEATURE_BANKS = ((4, 5), (6, 7), (4, 5), (0, 1))
SUM_BANKS = (2, 3, 6, 7, 4)
ALONE_BANKS = (5, 0, 1)
PRODUCT_TAGS = ("product", "w1_raw0", "w1_raw1")
TURNED_TAGS = ("turned", "tab_words0", "tab_words1")
SCORE_TAGS = ("w2_raw0", "w2_raw1", "w3_raw", "tab_words1")


def tile_list_zone_exposure_page_kernel(
    tc, tab_words, tab_scales, offs, offs2, offs3, w1, wind, page0, w4_words, w4_scales, w2, w3, level, out
):
    nc = tc.nc

    with ExitStack() as ctx:
        pool = ctx.enter_context(tc.tile_pool(name="sbuf", bufs=1))
        psum = ctx.enter_context(tc.psum_pool(name="psum", bufs=1))

        def sbuf(name, shape, dtype, tag=None):
            return pool.tile(shape, dtype, name=name, tag=tag or name, align_bytes=ALIGN)

        def bank(name, b):
            return psum.tile([P, BANK], F32, name=name, tag="bank%d" % b)

        def entries(list_tile, first, count):
            return list_tile[:, first // LIST_GROUP : (first + count) // LIST_GROUP]

        def load(name, shape, dtype, src, tag=None):
            t = sbuf(name, shape, dtype, tag)
            nc.sync.dma_start(out=t[:], in_=src)
            return t

        def load_rows(name, w, a):
            rows = w[a * K_PASS : (a + 1) * K_PASS, :]
            return load(name, [P, PACK, w.shape[1]], F32, rows.rearrange("(p j) c -> p j c", j=PACK))

        def load_words(a):
            src = tab_words[a].rearrange("p t i -> p (t i)").bitcast(I32)
            return load("tab_words%d" % a, [P, T], I32, src)

        page_rows = page0.rearrange("(p t) c -> t p c", t=PACK)
        wind_rows = wind.rearrange("(p t) j -> t p j", t=PACK)
        page = [None] * PACK
        wind_t = [None] * PACK

        def load_page(t):
            page[t] = load("page%d" % t, [P, T2], F32, page_rows[t])

        def load_wind(t):
            wind_t[t] = load("wind%d" % t, [P, S], F32, wind_rows[t])

        words0 = load_words(0)
        list1 = load("list1", [P, S // LIST_GROUP], U16, offs)
        tab_scale_rows = sbuf("tab_scale_rows", [P, T], U8)
        nc.vector.memset(tab_scale_rows[:].bitcast(I32), 0)
        for q in range(4):
            nc.sync.dma_start(
                out=tab_scale_rows[32 * q : 32 * q + 4 * PASSES, :].bitcast(I32),
                in_=tab_scales[:, 4 * q : 4 * q + 4, :].bitcast(I32),
            )
        w1_raw = [load_rows("w1_raw%d" % a, w1, a) for a in range(PASSES)]
        words1 = load_words(1)
        list2 = load("list2", [P, S // LIST_GROUP], U16, offs2)
        for t in range(PACK - 1):
            load_page(t)
            load_wind(t)
        load_wind(PACK - 1)
        list3 = load("list3", [P, PICK // LIST_GROUP], U16, offs3)
        w2_raw = [load_rows("w2_raw%d" % a, w2, a) for a in range(PASSES)]
        w3_raw = load_rows("w3_raw", w3, 0)
        w4_codes = load("w4_codes", [P, 2 * N], U8, w4_words[0])
        w4_scale_rows = sbuf("w4_scale_rows", [P, N], U8)
        nc.vector.memset(w4_scale_rows[:].bitcast(I32), 0)
        for q in range(4):
            nc.sync.dma_start(
                out=w4_scale_rows[32 * q : 32 * q + 4, :].bitcast(I32),
                in_=w4_scales[0, 4 * q : 4 * q + 4, :].bitcast(I32),
            )
        load_page(PACK - 1)
        with nc.allow_non_contiguous_dma(reason="one level value a partition and output tile"):
            level_cols = load("level_cols", [P, N // P], F32, level.rearrange("(i p) -> p i", p=P))

        halves = [slice(u * BANK, (u + 1) * BANK) for u in range(S // BANK)]
        v_codes = [sbuf("v_codes%d" % a, [P, S], U32) for a in range(PASSES)]
        v_scales = sbuf("v_scales", [P, S], U8)
        nc.vector.tensor_copy(out=v_codes[0][:], in_=words0[:].bitcast(U32).indirect(list1[:]))
        nc.vector.tensor_copy(out=v_scales[:], in_=tab_scale_rows[:].indirect(list1[:]))

        def v_operand(a, cols):
            return v_codes[a][:, cols].bitcast(FP8X4), v_scales[4 * a : P, cols]

        def quantize(codes, scales, grouped):
            nc.vector.quantize_mx(out=codes.bitcast(FP8X4), scales=scales, in_=grouped)

        w1_codes = [sbuf("w1_codes%d" % a, [P, H], U32) for a in range(PASSES)]
        w1_scales = [sbuf("w1_scales%d" % a, [P, H], U8) for a in range(PASSES)]

        def quantize_w1(a, copy):
            grouped = sbuf("w1_bf%d" % a, [P, PACK, P, PACK], BF16)
            copy(
                out=grouped[:].rearrange("p t m j -> p m j t"),
                in_=w1_raw[a][:].rearrange("p j (m t) -> p m j t", t=PACK),
            )
            quantize(w1_codes[a][:], w1_scales[a][:], grouped[:].rearrange("p t m j -> p (t m j)"))

        def quantize_weight(name, raw):
            codes = sbuf(name + "_codes", [P, N], U32)
            scales = sbuf(name + "_scales", [P, N], U8)
            for u in range(2):
                cols = slice(u * HALF_N, (u + 1) * HALF_N)
                grouped = sbuf("%s_bf%d" % (name, u), [P, HALF_N, PACK], BF16)
                nc.scalar.copy(
                    out=grouped[:].rearrange("p (c i) j -> p c j i", i=4),
                    in_=raw[:, :, cols].rearrange("p j (c i) -> p c j i", i=4),
                )
                quantize(codes[:, cols], scales[:, cols], grouped[:].rearrange("p c j -> p (c j)"))
            return codes, scales

        def fetch_standing(t):
            standing = sbuf("standing%d" % t, [P, S], F32, "standing%d" % (t % 2))
            nc.vector.tensor_copy(out=standing[:], in_=page[t][:].indirect(list2[:]))
            return standing

        identity = sbuf("identity", [P, P], F32)
        make_identity(nc, identity[:])

        def first_product(t, u, b):
            acc = bank("product%d_%d" % (t, u), b)
            for a in range(PASSES):
                rhs, rhs_scale = v_operand(a, halves[u])
                nc.tensor.matmul_mx(
                    out=acc[:],
                    lhsT=w1_codes[a][:, t * P : (t + 1) * P].bitcast(FP8X4),
                    lhsT_scale=w1_scales[a][:, t * P : (t + 1) * P],
                    rhs=rhs,
                    rhs_scale=rhs_scale,
                    start=(a == 0),
                    stop=(a == PASSES - 1),
                )
            return acc

        def feature_on_vector(t):
            feature = sbuf("feature%d" % t, [P, S], F32, "feature0")
            for u, cols in enumerate(halves):
                acc = first_product(t, u, FEATURE_BANKS[t][u])
                nc.vector.tensor_tensor(out=feature[:, cols], in0=acc[:], in1=wind_t[t][:, cols], op=ALU.add)
            return [feature[:, cols] for cols in halves]

        def feature_on_tensor(t):
            product = sbuf("product%d" % t, [P, S], F32, PRODUCT_TAGS[t - 1])
            turned = sbuf("turned%d" % t, [P, S], F32, TURNED_TAGS[t - 1])
            for u, cols in enumerate(halves):
                nc.scalar.copy(out=product[:, cols], in_=first_product(t, u, PRODUCT_BANKS[u])[:])
            for u, cols in enumerate(halves):
                acc = bank("turned%d_%d" % (t, u), TURNED_BANKS[u])
                for b in range(BANK // P):
                    block = slice(u * BANK + b * P, u * BANK + (b + 1) * P)
                    for term, first in ((product, True), (wind_t[t], False)):
                        nc.tensor.matmul(
                            acc[:, b * P : (b + 1) * P],
                            lhsT=term[:, block],
                            rhs=identity[:],
                            is_transpose=True,
                            start=first,
                            stop=not first,
                        )
                nc.scalar.copy(out=turned[:, cols], in_=acc[:])
            feature = []
            for u, cols in enumerate(halves):
                acc = bank("feature%d_%d" % (t, u), FEATURE_BANKS[t][u])
                for b in range(BANK // P):
                    block = slice(u * BANK + b * P, u * BANK + (b + 1) * P)
                    nc.tensor.transpose(acc[:, b * P : (b + 1) * P], turned[:, block], identity[:])
                feature.append(acc[:])
            return feature

        def update_page(t, standing, feature):
            larger = sbuf("larger%d" % t, [P, S], F32, "larger%d" % (t % 2))
            for u, cols in enumerate(halves):
                nc.vector.tensor_tensor(out=larger[:, cols], in0=feature[u], in1=standing[:, cols], op=ALU.max)
            nc.vector.tensor_copy(out=page[t][:].indirect(list2[:]), in_=larger[:])

        quantize_w1(0, nc.scalar.copy)
        quantize_w1(1, nc.scalar.copy)
        for u, cols in enumerate(halves):
            nc.vector.tensor_copy(
                out=v_codes[1][:, cols], in_=words1[:].bitcast(U32).indirect(entries(list1, u * BANK, BANK))
            )
        update_page(0, fetch_standing(0), feature_on_vector(0))
        features = {t: feature_on_tensor(t) for t in range(1, PACK)}
        for t in (1, 2):
            update_page(t, fetch_standing(t), features[t])
        w2_q = [quantize_weight("w2_%d" % a, w2_raw[a]) for a in range(PASSES)]
        w3_codes, w3_scales = quantize_weight("w3", w3_raw)
        update_page(3, fetch_standing(3), features[3])

        x_codes = sbuf("x_codes", [P, PICK], U32)
        x_scales = sbuf("x_scales", [P, PICK], U8)
        out_tiles = out.rearrange("(i p) j -> p i j", p=P)
        fetched = [None] * CHUNKS

        def fetch_zones(c):
            fetched[c] = sbuf("zones%d" % c, [P, PACK, CHUNK], F32, "larger%d" % (c % 2))
            for t in range(PACK):
                nc.vector.tensor_copy(out=fetched[c][:, t, :], in_=page[t][:].indirect(entries(list3, c * CHUNK, CHUNK)))

        def quantize_zones(c):
            cols = slice(c * CHUNK, (c + 1) * CHUNK)
            grouped = sbuf("x_bf%d" % c, [P, CHUNK, PACK], BF16, "x_bf%d" % (c % 2))
            copy = nc.scalar.copy if c in (0, 1) else nc.vector.tensor_copy
            copy(
                out=grouped[:].rearrange("p (c i) t -> p c t i", i=4),
                in_=fetched[c][:].rearrange("p t (c i) -> p c t i", i=4),
            )
            quantize(x_codes[:, cols], x_scales[:, cols], grouped[:].rearrange("p c t -> p (c t)"))

        open_sums = []

        def open_sum(unit):
            c, pair = divmod(unit, PAIRS)
            together = bank("together%d" % unit, SUM_BANKS[unit % len(SUM_BANKS)])
            for e in range(2):
                n_cols = slice((2 * pair + e) * P, (2 * pair + e + 1) * P)
                for a in range(PASSES):
                    rhs, rhs_scale = v_operand(a, slice(c * CHUNK, (c + 1) * CHUNK))
                    nc.tensor.matmul_mx(
                        out=together[:, e * CHUNK : (e + 1) * CHUNK],
                        lhsT=w2_q[a][0][:, n_cols].bitcast(FP8X4),
                        lhsT_scale=w2_q[a][1][:, n_cols],
                        rhs=rhs,
                        rhs_scale=rhs_scale,
                        start=(e == 0 and a == 0),
                        stop=False,
                    )
            open_sums.append(together)

        def score(c):
            cols = slice(c * CHUNK, (c + 1) * CHUNK)
            x_operand = x_codes[:, cols].bitcast(FP8X4)
            scores = sbuf("scores%d" % c, [P, 2, PAIRS, BANK], F32, SCORE_TAGS[c])
            for pair in range(PAIRS):
                unit = c * PAIRS + pair
                if unit == len(open_sums):
                    open_sum(unit)
                together = open_sums[unit]
                alone = bank("alone%d" % unit, ALONE_BANKS[unit % len(ALONE_BANKS)])
                for e in range(2):
                    i = 2 * pair + e
                    nc.tensor.matmul_mx(
                        out=together[:, e * CHUNK : (e + 1) * CHUNK],
                        lhsT=w4_codes[:, 2 * i * P : 2 * (i + 1) * P].bitcast(FP4X4),
                        lhsT_scale=w4_scale_rows[:, i * P : (i + 1) * P],
                        rhs=x_operand,
                        rhs_scale=x_scales[:, cols],
                        start=False,
                        stop=(e == 1),
                    )
                for e in range(2):
                    i = 2 * pair + e
                    nc.tensor.matmul_mx(
                        out=alone[:, e * CHUNK : (e + 1) * CHUNK],
                        lhsT=w3_codes[:, i * P : (i + 1) * P].bitcast(FP8X4),
                        lhsT_scale=w3_scales[:, i * P : (i + 1) * P],
                        rhs=x_operand,
                        rhs_scale=x_scales[:, cols],
                        start=True,
                        stop=True,
                    )
                tanh_together = scores[:, 0, pair, :]
                tanh_alone = scores[:, 1, pair, :]
                nc.scalar.activation(out=tanh_together, in_=together[:], func=ACT.Tanh)
                for e in range(2):
                    i = 2 * pair + e
                    nc.scalar.activation(
                        out=tanh_alone[:, e * CHUNK : (e + 1) * CHUNK],
                        in_=alone[:, e * CHUNK : (e + 1) * CHUNK],
                        func=ACT.Tanh,
                        bias=level_cols[:, i : i + 1],
                    )
                step = 1 if unit == CHUNKS * PAIRS - 1 else 2
                for e in range(0, 2, step):
                    tiles = slice(2 * pair + e, 2 * pair + e + step)
                    part = slice(e * CHUNK, (e + step) * CHUNK)
                    nc.vector.tensor_tensor(
                        out=tanh_together[:, part],
                        in0=tanh_together[:, part],
                        in1=tanh_alone[:, part],
                        op=ALU.max,
                    )
                    nc.sync.dma_start(
                        out=out_tiles[:, tiles, cols],
                        in_=tanh_together[:, part].rearrange("p (e j) -> p e j", j=CHUNK),
                    )

        for unit in range(len(SUM_BANKS)):
            open_sum(unit)
        for c in range(CHUNKS + 1):
            if c < CHUNKS:
                fetch_zones(c)
                quantize_zones(c)
            if c >= 1:
                score(c - 1)
